import numpy as np
import ml_dtypes


def mxq(x, axis, fmt="e4m3"):
    dtype, down = {"e4m3": (ml_dtypes.float8_e4m3fn, 7), "e5m2": (ml_dtypes.float8_e5m2, 14)}[fmt]
    v = np.moveaxis(np.asarray(x, np.float32).astype(ml_dtypes.bfloat16).astype(np.float64), axis, -1)
    blocks = v.reshape(v.shape[:-1] + (-1, 32))
    amax = np.abs(blocks).max(-1, keepdims=True)
    byte = np.maximum(np.where(amax > 0, np.frexp(amax)[1] - 1 + 127, 0) - down, 1)
    scale = np.exp2(byte - 127.0)
    codes = (blocks / scale).astype(np.float32).astype(dtype).astype(np.float64)
    return np.moveaxis((codes * scale).reshape(v.shape), -1, axis)


WIDE = False


def mx_kscale(k):
    if not WIDE:
        return np.ones(k)
    levels = np.array([10, -10, 5, -5, 0])
    if k % 512:
        return np.exp2(np.random.permutation(np.resize(levels, k // 32))).repeat(32)
    a = np.empty((k // 512, 16))
    for p in range(k // 512):
        a[p, :8] = np.random.permutation(np.resize(levels, 8))
        for g in range(8):
            far = levels[np.abs(levels - a[p, g]) >= 10]
            a[p, g + 8] = far[np.random.randint(len(far))]
    return np.exp2(a.ravel()).repeat(32)


def f64(x):
    return np.asarray(x).astype(np.float64)


def striped(idx):
    return np.tile(idx.reshape(-1, 16).T, (8, 1)).astype(np.uint16)


def unstriped(offs):
    return offs[:16].T.reshape(-1).astype(np.int64)


E2M1 = np.array([0.0, 0.5, 1.0, 1.5, 2.0, 3.0, 4.0, 6.0, -0.0, -0.5, -1.0, -1.5, -2.0, -3.0, -4.0, -6.0])


def pack_weight(w, fmt):
    k, n = w.shape
    w = f64(np.asarray(w, np.float32).astype(ml_dtypes.bfloat16)).reshape(k // 32, 32, n)
    amax = np.abs(w).max(1)
    if fmt == "e4m3":
        byte = np.frexp(amax)[1] - 1 + 127 - 7
    else:
        mant, ex = np.frexp(amax / 6.0)
        byte = np.where(mant > 0.5, ex, ex - 1) + 127
    byte = np.clip(np.where(amax > 0, byte, 1), 1, 254)
    scaled = (w * np.exp2(127.0 - byte)[:, None, :]).reshape(k, n).astype(np.float32)
    by_word = np.ascontiguousarray(scaled.reshape(k // 512, 128, 4, n).transpose(0, 1, 3, 2))
    if fmt == "e4m3":
        words = by_word.astype(ml_dtypes.float8_e4m3fn).view(np.uint8)
    else:
        c = by_word.astype(ml_dtypes.float4_e2m1fn).view(np.uint8) & 0xF
        words = (c[..., 0::2] | (c[..., 1::2] << 4)).reshape(k // 512, 128, 2 * n)
    return np.ascontiguousarray(words), np.ascontiguousarray(byte.astype(np.uint8).reshape(k // 512, 16, n))


def unpack_weight(words, scales, fmt):
    g, _, n = scales.shape
    words = np.ascontiguousarray(words).reshape(g, 128, n, -1)
    if fmt == "e4m3":
        vals = words.view(ml_dtypes.float8_e4m3fn).astype(np.float64)
    else:
        nib = np.empty((g, 128, n, 4), np.uint8)
        nib[..., 0::2] = words & 0xF
        nib[..., 1::2] = words >> 4
        vals = E2M1[nib]
    vals = vals * np.repeat(np.exp2(scales.astype(np.float64) - 127.0), 8, axis=1)[..., None]
    return vals.transpose(0, 1, 3, 2).reshape(g * 512, n)


def gelu(v):
    return 0.5 * v * (1.0 + np.tanh(np.sqrt(2.0 / np.pi) * (v + 0.044715 * v**3)))


K, H, T, S, N, P1, P2, P3 = 1024, 512, 4096, 2048, 1024, 1024, 512, 256

def setup_inputs():
    n = np.random.standard_normal
    s = mx_kscale(K)[:, None]
    u = mx_kscale(H)[:, None]
    tab_words, tab_scales = pack_weight(n((K, T)) * s, "e4m3")
    w2_words, w2_scales = pack_weight(0.8 * n((H, N)) / np.sqrt(H) / u, "e2m1")
    return {
        "tab_words": tab_words,
        "tab_scales": tab_scales,
        "offs": striped(np.random.permutation(T)[:S]),
        "w1": (1.5 * n((K, H)) / np.sqrt(K) / s).astype(np.float32),
        "pos1": striped(np.random.permutation(S)[:P1]),
        "pos2": striped(np.random.permutation(S)[:P1]),
        "gain": (np.exp(0.3 * n(H)) * u[:, 0]).astype(np.float32),
        "pos3": striped(np.random.permutation(P1)[:P2]),
        "pos4": striped(np.random.permutation(P1)[:P2]),
        "pos5": striped(np.random.permutation(P2)[:P3]),
        "pos6": striped(np.random.permutation(P2)[:P3]),
        "lean": np.exp(0.4 * n(H)).astype(np.float32),
        "w2_words": w2_words,
        "w2_scales": w2_scales,
    }

def reference(tab_words, tab_scales, offs, w1, pos1, pos2, gain, pos3, pos4, pos5, pos6, lean, w2_words, w2_scales):
    v = unpack_weight(tab_words, tab_scales, "e4m3")[:, unstriped(offs)]
    x = mxq(f64(w1), 0, "e4m3").T @ v
    h = 0.5 * x * (1.0 + np.tanh(0.7978845608 * (x + 0.044715 * x ** 3)))
    a1 = f64(gain)[:, None] * (h[:, unstriped(pos1)] * h[:, unstriped(pos2)])
    a2 = a1[:, unstriped(pos3)] - a1[:, unstriped(pos4)]
    a3 = np.maximum(a2[:, unstriped(pos5)], f64(lean)[:, None] * a2[:, unstriped(pos6)])
    w2 = unpack_weight(w2_words, w2_scales, "e2m1")
    y = w2.T @ mxq(a3, 0, "e4m3")
    return np.tanh(y)

@@ -1,0 +1,233 @@
+from contextlib import ExitStack
+
+import concourse.mybir as mybir
+
+K, H, T, S, N, P1, P2, P3 = 1024, 512, 4096, 2048, 1024, 1024, 512, 256
+FLOPS = 2 * K * H * S + 2 * H * N * P3
+
+F32 = mybir.dt.float32
+BF16 = mybir.dt.bfloat16
+I32 = mybir.dt.int32
+U32 = mybir.dt.uint32
+U16 = mybir.dt.uint16
+U8 = mybir.dt.uint8
+FP8X4 = mybir.dt.float8_e4m3fn_x4
+FP4X4 = mybir.dt.float4_e2m1fn_x4
+ACT = mybir.ActivationFunctionType
+ALU = mybir.AluOpType
+
+P = 128
+PACK = 4
+CHUNK = 512
+CHUNKS = S // CHUNK
+HALF = P3 // 2
+
+
+def tile_list_residency_ranking_scores_kernel(
+    tc, tab_words, tab_scales, offs, w1, pos1, pos2, gain, pos3, pos4, pos5, pos6, lean, w2_words, w2_scales, out
+):
+    nc = tc.nc
+    with ExitStack() as ctx:
+        lists = ctx.enter_context(tc.tile_pool(name="lists", bufs=1))
+        keep = ctx.enter_context(tc.tile_pool(name="keep", bufs=1))
+        shared = ctx.enter_context(tc.tile_pool(name="shared", bufs=1))
+        psum = ctx.enter_context(tc.psum_pool(name="psum", bufs=8))
+
+        def load_list(src, name):
+            tile = lists.tile([P, src.shape[1]], U16, name=name)
+            nc.sync.dma_start(tile[:], src)
+            return tile
+
+        def load_words(a, tile):
+            nc.sync.dma_start(tile[:].bitcast(I32), tab_words[a].rearrange("p n i -> p (n i)").bitcast(I32))
+
+        idx = load_list(offs, "idx")
+        scale_table = shared.tile([P, T], U8, name="scale_table", offset=14336, align_bytes=64)
+        nc.sync.dma_start(
+            scale_table[0:32, :].bitcast(I32), tab_scales.rearrange("a q t -> (a q) t").bitcast(I32)
+        )
+        nc.vector.memset(scale_table[32:64, :].bitcast(I32), 0)
+        nc.vector.memset(scale_table[64:128, :].bitcast(I32), 0)
+        words0 = keep.tile([P, T], U32, name="words0", align_bytes=64)
+        load_words(0, words0)
+        p1 = load_list(pos1, "p1")
+        p2 = load_list(pos2, "p2")
+        p3 = load_list(pos3, "p3")
+        p4 = load_list(pos4, "p4")
+        p5 = load_list(pos5, "p5")
+        p6 = load_list(pos6, "p6")
+        w1_raw0 = keep.tile([P, 1, PACK, H], F32, name="w1_raw0")
+        nc.sync.dma_start(w1_raw0[:, 0], w1[0:512, :].rearrange("(p j) c -> p j c", j=PACK))
+
+        planes = [keep.tile([P, S], U8, name="plane%d" % a, align_bytes=64) for a in range(2)]
+        for plane in planes:
+            nc.gpsimd.memset(plane[:].bitcast(I32), 0)
+
+        picked_scales = keep.tile([P, S], U8, name="picked_scales", align_bytes=64)
+        nc.vector.tensor_copy(picked_scales[:], scale_table[:].indirect(idx[:]))
+
+        def move_planes(a):
+            for q in range(4):
+                nc.sync.dma_start(
+                    planes[a][32 * q : 32 * q + 4, :].bitcast(I32),
+                    picked_scales[16 * a + 4 * q : 16 * a + 4 * q + 4, :].bitcast(I32),
+                )
+
+        words1 = shared.tile([P, T], U32, name="words1", offset=0, align_bytes=64)
+        load_words(1, words1)
+        move_planes(0)
+        w1_raw1 = shared.tile([P, 2, PACK, H // 2], F32, name="w1_raw1", offset=16384, align_bytes=64)
+        for half in range(2):
+            nc.sync.dma_start(
+                w1_raw1[:, half],
+                w1[512:1024, 256 * half : 256 * half + 256].rearrange("(p j) c -> p j c", j=PACK),
+            )
+        move_planes(1)
+
+        picked = {}
+
+        def pick_words(a, c, window, tile):
+            nc.vector.tensor_copy(tile[:], window[:].indirect(idx[:, 32 * c : 32 * c + 32]))
+            picked[(a, c)] = tile
+
+        def round_w1(raw, rounded):
+            pieces = raw.shape[1]
+            m_piece = P // pieces
+            for piece in range(pieces):
+                nc.scalar.copy(
+                    rounded[:, :, m_piece * piece : m_piece * (piece + 1), :].rearrange("p t m j -> p m j t"),
+                    raw[:, piece].rearrange("p j (m t) -> p m j t", t=PACK),
+                )
+
+        def quantize_w1(a, t0, t1):
+            nc.vector.quantize_mx(
+                out=w1_codes[a][:, P * t0 : P * t1].bitcast(FP8X4),
+                scales=w1_scales[a][:, P * t0 : P * t1],
+                in_=w1_bf[a][:, t0:t1].rearrange("p t m j -> p (t m j)"),
+            )
+
+        w1_bf = [keep.tile([P, PACK, P, PACK], BF16, name="w1_bf%d" % a, align_bytes=64) for a in range(2)]
+        w1_codes = [keep.tile([P, H], U32, name="w1_codes%d" % a, align_bytes=64) for a in range(2)]
+        w1_scales = [keep.tile([P, H], U8, name="w1_scales%d" % a, align_bytes=64) for a in range(2)]
+
+        for c in range(CHUNKS):
+            pick_words(0, c, words0, keep.tile([P, CHUNK], U32, name="picked0_%d" % c, align_bytes=64))
+        round_w1(w1_raw0, w1_bf[0])
+        quantize_w1(0, 0, 4)
+        for c in range(CHUNKS - 1):
+            pick_words(1, c, words1, keep.tile([P, CHUNK], U32, name="picked1_%d" % c, align_bytes=64))
+        round_w1(w1_raw1, w1_bf[1])
+        quantize_w1(1, 0, 1)
+        pick_words(1, CHUNKS - 1, words1, shared.tile([P, CHUNK], U32, name="picked1_last", offset=20480, align_bytes=64))
+        quantize_w1(1, 1, 4)
+
+        gain_sb = shared.tile([P, PACK], F32, name="gain_sb", offset=0, align_bytes=64)
+        nc.sync.dma_start(gain_sb[:], gain.rearrange("(p t) -> p t", t=PACK))
+        lean_sb = shared.tile([P, PACK], F32, name="lean_sb", offset=64, align_bytes=64)
+        nc.sync.dma_start(lean_sb[:], lean.rearrange("(p t) -> p t", t=PACK))
+        w2_codes = shared.tile([P, 2 * N], U8, name="w2_codes", offset=1024, align_bytes=64)
+        nc.sync.dma_start(w2_codes[:].bitcast(I32), w2_words[0].bitcast(I32))
+        w2_plane = shared.tile([P, N], U8, name="w2_plane", offset=4096, align_bytes=64)
+        nc.gpsimd.memset(w2_plane[:].bitcast(I32), 0)
+        for q in range(4):
+            nc.sync.dma_start(
+                w2_plane[32 * q : 32 * q + 4, :].bitcast(I32), w2_scales[0, 4 * q : 4 * q + 4, :].bitcast(I32)
+            )
+
+        def first_pass(acc, a, t, c):
+            nc.tensor.matmul_mx(
+                out=acc[:],
+                lhsT=w1_codes[a][:, P * t : P * (t + 1)].bitcast(FP8X4),
+                lhsT_scale=w1_scales[a][:, P * t : P * (t + 1)],
+                rhs=picked[(a, c)][:].bitcast(FP8X4),
+                rhs_scale=planes[a][:, CHUNK * c : CHUNK * (c + 1)],
+                start=(a == 0),
+                stop=(a == 1),
+            )
+
+        h = [keep.tile([P, S], F32, name="h%d" % t) for t in range(PACK)]
+        left = [keep.tile([P, P1], F32, name="left%d" % t) for t in range(PACK)]
+        gained = [keep.tile([P, P1], F32, name="gained%d" % t) for t in range(PACK)]
+        a1 = [keep.tile([P, P1], F32, name="a1_%d" % t) for t in range(PACK)]
+        minus = [keep.tile([P, P2], F32, name="minus%d" % t) for t in range(PACK)]
+        a2 = [keep.tile([P, P2], F32, name="a2_%d" % t) for t in range(PACK)]
+        hosp_l = [keep.tile([P, P3], F32, name="hosp_l%d" % t) for t in range(PACK)]
+        hosp_r = [keep.tile([P, P3], F32, name="hosp_r%d" % t) for t in range(PACK)]
+        a3 = keep.tile([P, PACK, P3], F32, name="a3")
+        a3_bf = [keep.tile([P, HALF, PACK], BF16, name="a3_bf%d" % u, align_bytes=64) for u in range(2)]
+        a3_codes = [keep.tile([P, HALF], U32, name="a3_codes%d" % u, align_bytes=64) for u in range(2)]
+        a3_scales = [keep.tile([P, HALF], U8, name="a3_scales%d" % u, align_bytes=64) for u in range(2)]
+
+        def larger(dst, t, cols):
+            nc.vector.scalar_tensor_tensor(
+                dst, hosp_r[t][:, cols], lean_sb[:, t : t + 1], hosp_l[t][:, cols], ALU.mult, ALU.max
+            )
+
+        def scores(u):
+            nc.vector.quantize_mx(
+                out=a3_codes[u][:].bitcast(FP8X4),
+                scales=a3_scales[u][:],
+                in_=a3_bf[u][:].rearrange("p m t -> p (m t)"),
+            )
+            for g in range(2):
+                acc = psum.tile([P, 4, HALF], F32, name="acc", tag="acc")
+                for j in range(4):
+                    n0 = P * (4 * g + j)
+                    nc.tensor.matmul_mx(
+                        out=acc[:, j, :],
+                        lhsT=w2_codes[:, 2 * n0 : 2 * (n0 + P)].bitcast(FP4X4),
+                        lhsT_scale=w2_plane[:, n0 : n0 + P],
+                        rhs=a3_codes[u][:].bitcast(FP8X4),
+                        rhs_scale=a3_scales[u][:],
+                        start=True,
+                        stop=True,
+                    )
+                res = keep.tile([P, 4, HALF], F32, name="res%d_%d" % (u, g))
+                nc.scalar.activation(res[:], acc[:], ACT.Tanh)
+                nc.sync.dma_start(
+                    out[512 * g : 512 * (g + 1), HALF * u : HALF * (u + 1)].rearrange("(j p) m -> p j m", p=P),
+                    res[:],
+                )
+
+        for pair in ((0, 1), (2, 3)):
+            accs = {}
+            for t in pair:
+                for c in range(CHUNKS):
+                    accs[(t, c)] = psum.tile([P, CHUNK], F32, name="acc", tag="acc")
+                    first_pass(accs[(t, c)], 0, t, c)
+            for t in pair:
+                for c in range(CHUNKS):
+                    first_pass(accs[(t, c)], 1, t, c)
+                    nc.scalar.activation(h[t][:, CHUNK * c : CHUNK * (c + 1)], accs[(t, c)][:], ACT.Gelu_apprx_tanh)
+            for t in pair:
+                nc.vector.tensor_copy(left[t][:], h[t][:].indirect(p1[:]))
+                nc.scalar.activation(gained[t][:], left[t][:], ACT.Copy, scale=gain_sb[:, t : t + 1])
+            for t in pair:
+                nc.vector.tensor_tensor(a1[t][:], h[t][:].indirect(p2[:]), gained[t][:], ALU.mult)
+            for t in pair:
+                nc.vector.tensor_copy(minus[t][:], a1[t][:].indirect(p4[:]))
+            for t in pair:
+                nc.vector.tensor_tensor(a2[t][:], a1[t][:].indirect(p3[:]), minus[t][:], ALU.subtract)
+            if pair[0] == 0:
+                for t in pair:
+                    nc.vector.tensor_copy(hosp_r[t][:], a2[t][:].indirect(p6[:]))
+                    nc.vector.tensor_copy(hosp_l[t][:], a2[t][:].indirect(p5[:]))
+                for t in pair:
+                    larger(a3[:, t, :], t, slice(0, P3))
+                nc.scalar.copy(a3_bf[1][:, :, 0:2], a3[:, 0:2, HALF:P3].rearrange("p t m -> p m t"))
+            else:
+                for u in range(2):
+                    cols = slice(HALF * u, HALF * (u + 1))
+                    lcols = slice(8 * u, 8 * u + 8)
+                    for t in pair:
+                        nc.vector.tensor_copy(hosp_r[t][:, cols], a2[t][:].indirect(p6[:, lcols]))
+                        nc.vector.tensor_copy(hosp_l[t][:, cols], a2[t][:].indirect(p5[:, lcols]))
+                    for t in pair:
+                        if u == 0:
+                            larger(a3[:, t, cols], t, cols)
+                        else:
+                            larger(a3_bf[1][:, :, t], t, cols)
+                    if u == 0:
+                        nc.scalar.copy(a3_bf[0][:], a3[:, :, cols].rearrange("p t m -> p m t"))
+                for u in range(2):
+                    scores(u)

@@ -21,6 +21,7 @@ PACK = 4
 CHUNK = 512
 CHUNKS = S // CHUNK
 HALF = P3 // 2
+GROUP = 2
 
 
 def tile_list_residency_ranking_scores_kernel(
@@ -31,6 +32,7 @@ def tile_list_residency_ranking_scores_kernel(
         lists = ctx.enter_context(tc.tile_pool(name="lists", bufs=1))
         keep = ctx.enter_context(tc.tile_pool(name="keep", bufs=1))
         shared = ctx.enter_context(tc.tile_pool(name="shared", bufs=1))
+        late = ctx.enter_context(tc.tile_pool(name="late", bufs=1))
         psum = ctx.enter_context(tc.psum_pool(name="psum", bufs=8))
 
         def load_list(src, name):
@@ -88,7 +90,7 @@ def tile_list_residency_ranking_scores_kernel(
 
         def pick_words(a, c, window, tile):
             nc.vector.tensor_copy(tile[:], window[:].indirect(idx[:, 32 * c : 32 * c + 32]))
-            picked[(a, c)] = tile
+            picked[(a, c)] = tile[:]
 
         def round_w1(raw, rounded):
             pieces = raw.shape[1]
@@ -110,8 +112,10 @@ def tile_list_residency_ranking_scores_kernel(
         w1_codes = [keep.tile([P, H], U32, name="w1_codes%d" % a, align_bytes=64) for a in range(2)]
         w1_scales = [keep.tile([P, H], U8, name="w1_scales%d" % a, align_bytes=64) for a in range(2)]
 
+        picked0 = keep.tile([P, S], U32, name="picked0", align_bytes=64)
+        nc.vector.tensor_copy(picked0[:], words0[:].indirect(idx[:]))
         for c in range(CHUNKS):
-            pick_words(0, c, words0, keep.tile([P, CHUNK], U32, name="picked0_%d" % c, align_bytes=64))
+            picked[(0, c)] = picked0[:, CHUNK * c : CHUNK * (c + 1)]
         round_w1(w1_raw0, w1_bf[0])
         quantize_w1(0, 0, 4)
         for c in range(CHUNKS - 1):
@@ -128,7 +132,7 @@ def tile_list_residency_ranking_scores_kernel(
         w2_codes = shared.tile([P, 2 * N], U8, name="w2_codes", offset=1024, align_bytes=64)
         nc.sync.dma_start(w2_codes[:].bitcast(I32), w2_words[0].bitcast(I32))
         w2_plane = shared.tile([P, N], U8, name="w2_plane", offset=4096, align_bytes=64)
-        nc.gpsimd.memset(w2_plane[:].bitcast(I32), 0)
+        nc.vector.memset(w2_plane[:].bitcast(I32), 0)
         for q in range(4):
             nc.sync.dma_start(
                 w2_plane[32 * q : 32 * q + 4, :].bitcast(I32), w2_scales[0, 4 * q : 4 * q + 4, :].bitcast(I32)
@@ -139,7 +143,7 @@ def tile_list_residency_ranking_scores_kernel(
                 out=acc[:],
                 lhsT=w1_codes[a][:, P * t : P * (t + 1)].bitcast(FP8X4),
                 lhsT_scale=w1_scales[a][:, P * t : P * (t + 1)],
-                rhs=picked[(a, c)][:].bitcast(FP8X4),
+                rhs=picked[(a, c)].bitcast(FP8X4),
                 rhs_scale=planes[a][:, CHUNK * c : CHUNK * (c + 1)],
                 start=(a == 0),
                 stop=(a == 1),
@@ -149,18 +153,31 @@ def tile_list_residency_ranking_scores_kernel(
         left = [keep.tile([P, P1], F32, name="left%d" % t) for t in range(PACK)]
         gained = [keep.tile([P, P1], F32, name="gained%d" % t) for t in range(PACK)]
         a1 = [keep.tile([P, P1], F32, name="a1_%d" % t) for t in range(PACK)]
-        minus = [keep.tile([P, P2], F32, name="minus%d" % t) for t in range(PACK)]
+        minus = [late.tile([P, P2], F32, name="minus%d" % t, offset=2048 * t) for t in range(PACK)]
         a2 = [keep.tile([P, P2], F32, name="a2_%d" % t) for t in range(PACK)]
-        hosp_l = [keep.tile([P, P3], F32, name="hosp_l%d" % t) for t in range(PACK)]
-        hosp_r = [keep.tile([P, P3], F32, name="hosp_r%d" % t) for t in range(PACK)]
-        a3 = keep.tile([P, PACK, P3], F32, name="a3")
+        a3_lo = late.tile([P, PACK, HALF], F32, name="a3_lo", offset=8192)
+        a3_hi = keep.tile([P, 2, HALF], F32, name="a3_hi")
         a3_bf = [keep.tile([P, HALF, PACK], BF16, name="a3_bf%d" % u, align_bytes=64) for u in range(2)]
         a3_codes = [keep.tile([P, HALF], U32, name="a3_codes%d" % u, align_bytes=64) for u in range(2)]
         a3_scales = [keep.tile([P, HALF], U8, name="a3_scales%d" % u, align_bytes=64) for u in range(2)]
 
-        def larger(dst, t, cols):
+        hosp = {}
+
+        def pick_hospitals(t, u):
+            cols = slice(8 * u, 8 * u + 8)
+            for side, places in enumerate((p6, p5)):
+                name = "hosp%d_%d_%d" % (t, u, side)
+                if u == 0:
+                    tile = keep.tile([P, HALF], F32, name=name)
+                else:
+                    base = 2048 * 3 if t < 2 else 8192
+                    tile = late.tile([P, HALF], F32, name=name, offset=base + 512 * (2 * (t % 2) + side))
+                nc.vector.tensor_copy(tile[:], a2[t][:].indirect(places[:, cols]))
+                hosp[(t, u, side)] = tile
+
+        def larger(dst, t, u):
             nc.vector.scalar_tensor_tensor(
-                dst, hosp_r[t][:, cols], lean_sb[:, t : t + 1], hosp_l[t][:, cols], ALU.mult, ALU.max
+                dst, hosp[(t, u, 0)][:], lean_sb[:, t : t + 1], hosp[(t, u, 1)][:], ALU.mult, ALU.max
             )
 
         def scores(u):
@@ -169,10 +186,10 @@ def tile_list_residency_ranking_scores_kernel(
                 scales=a3_scales[u][:],
                 in_=a3_bf[u][:].rearrange("p m t -> p (m t)"),
             )
-            for g in range(2):
-                acc = psum.tile([P, 4, HALF], F32, name="acc", tag="acc")
-                for j in range(4):
-                    n0 = P * (4 * g + j)
+            for g in range(N // (P * GROUP)):
+                acc = psum.tile([P, GROUP, HALF], F32, name="acc", tag="acc")
+                for j in range(GROUP):
+                    n0 = P * (GROUP * g + j)
                     nc.tensor.matmul_mx(
                         out=acc[:, j, :],
                         lhsT=w2_codes[:, 2 * n0 : 2 * (n0 + P)].bitcast(FP4X4),
@@ -182,10 +199,10 @@ def tile_list_residency_ranking_scores_kernel(
                         start=True,
                         stop=True,
                     )
-                res = keep.tile([P, 4, HALF], F32, name="res%d_%d" % (u, g))
+                res = keep.tile([P, GROUP, HALF], F32, name="res%d_%d" % (u, g))
                 nc.scalar.activation(res[:], acc[:], ACT.Tanh)
                 nc.sync.dma_start(
-                    out[512 * g : 512 * (g + 1), HALF * u : HALF * (u + 1)].rearrange("(j p) m -> p j m", p=P),
+                    out[P * GROUP * g : P * GROUP * (g + 1), HALF * u : HALF * (u + 1)].rearrange("(j p) m -> p j m", p=P),
                     res[:],
                 )
 
@@ -208,26 +225,19 @@ def tile_list_residency_ranking_scores_kernel(
                 nc.vector.tensor_copy(minus[t][:], a1[t][:].indirect(p4[:]))
             for t in pair:
                 nc.vector.tensor_tensor(a2[t][:], a1[t][:].indirect(p3[:]), minus[t][:], ALU.subtract)
-            if pair[0] == 0:
-                for t in pair:
-                    nc.vector.tensor_copy(hosp_r[t][:], a2[t][:].indirect(p6[:]))
-                    nc.vector.tensor_copy(hosp_l[t][:], a2[t][:].indirect(p5[:]))
-                for t in pair:
-                    larger(a3[:, t, :], t, slice(0, P3))
-                nc.scalar.copy(a3_bf[1][:, :, 0:2], a3[:, 0:2, HALF:P3].rearrange("p t m -> p m t"))
-            else:
-                for u in range(2):
-                    cols = slice(HALF * u, HALF * (u + 1))
-                    lcols = slice(8 * u, 8 * u + 8)
-                    for t in pair:
-                        nc.vector.tensor_copy(hosp_r[t][:, cols], a2[t][:].indirect(p6[:, lcols]))
-                        nc.vector.tensor_copy(hosp_l[t][:, cols], a2[t][:].indirect(p5[:, lcols]))
-                    for t in pair:
-                        if u == 0:
-                            larger(a3[:, t, cols], t, cols)
-                        else:
-                            larger(a3_bf[1][:, :, t], t, cols)
-                    if u == 0:
-                        nc.scalar.copy(a3_bf[0][:], a3[:, :, cols].rearrange("p t m -> p m t"))
-                for u in range(2):
-                    scores(u)
+            for t in pair:
+                pick_hospitals(t, 0)
+            for t in pair:
+                larger(a3_lo[:, t, :], t, 0)
+        nc.scalar.copy(a3_bf[0][:], a3_lo[:].rearrange("p t m -> p m t"))
+        for t in (0, 1):
+            pick_hospitals(t, 1)
+        for t in (0, 1):
+            larger(a3_hi[:, t, :], t, 1)
+        nc.scalar.copy(a3_bf[1][:, :, 0:2], a3_hi[:].rearrange("p t m -> p m t"))
+        scores(0)
+        for t in (2, 3):
+            pick_hospitals(t, 1)
+        for t in (2, 3):
+            larger(a3_bf[1][:, :, t], t, 1)
+        scores(1)

@@ -44,7 +44,7 @@ def tile_list_residency_ranking_scores_kernel(
             nc.sync.dma_start(tile[:].bitcast(I32), tab_words[a].rearrange("p n i -> p (n i)").bitcast(I32))
 
         idx = load_list(offs, "idx")
-        scale_table = shared.tile([P, T], U8, name="scale_table", offset=14336, align_bytes=64)
+        scale_table = keep.tile([P, T], U8, name="scale_table", align_bytes=64)
         nc.sync.dma_start(
             scale_table[0:32, :].bitcast(I32), tab_scales.rearrange("a q t -> (a q) t").bitcast(I32)
         )
@@ -52,14 +52,22 @@ def tile_list_residency_ranking_scores_kernel(
         nc.vector.memset(scale_table[64:128, :].bitcast(I32), 0)
         words0 = keep.tile([P, T], U32, name="words0", align_bytes=64)
         load_words(0, words0)
+        w1_raw0 = keep.tile([P, 1, PACK, H], F32, name="w1_raw0")
+        nc.sync.dma_start(w1_raw0[:, 0], w1[0:512, :].rearrange("(p j) c -> p j c", j=PACK))
+        words1 = shared.tile([P, T], U32, name="words1", offset=0, align_bytes=64)
+        load_words(1, words1)
+        w1_raw1 = shared.tile([P, 2, PACK, H // 2], F32, name="w1_raw1", offset=16384, align_bytes=64)
+        for half in range(2):
+            nc.sync.dma_start(
+                w1_raw1[:, half],
+                w1[512:1024, 256 * half : 256 * half + 256].rearrange("(p j) c -> p j c", j=PACK),
+            )
         p1 = load_list(pos1, "p1")
         p2 = load_list(pos2, "p2")
         p3 = load_list(pos3, "p3")
         p4 = load_list(pos4, "p4")
         p5 = load_list(pos5, "p5")
         p6 = load_list(pos6, "p6")
-        w1_raw0 = keep.tile([P, 1, PACK, H], F32, name="w1_raw0")
-        nc.sync.dma_start(w1_raw0[:, 0], w1[0:512, :].rearrange("(p j) c -> p j c", j=PACK))
 
         planes = [keep.tile([P, S], U8, name="plane%d" % a, align_bytes=64) for a in range(2)]
         for plane in planes:
@@ -67,24 +75,12 @@ def tile_list_residency_ranking_scores_kernel(
 
         picked_scales = keep.tile([P, S], U8, name="picked_scales", align_bytes=64)
         nc.vector.tensor_copy(picked_scales[:], scale_table[:].indirect(idx[:]))
-
-        def move_planes(a):
-            for q in range(4):
-                nc.sync.dma_start(
-                    planes[a][32 * q : 32 * q + 4, :].bitcast(I32),
-                    picked_scales[16 * a + 4 * q : 16 * a + 4 * q + 4, :].bitcast(I32),
+        for a, queue in enumerate((nc.gpsimd, nc.sync)):
+            for r in range(4):
+                queue.dma_start(
+                    planes[a][4 * a + r : P : 32, :].bitcast(I32),
+                    picked_scales[16 * a + r : 16 * a + 16 : 4, :].bitcast(I32),
                 )
-
-        words1 = shared.tile([P, T], U32, name="words1", offset=0, align_bytes=64)
-        load_words(1, words1)
-        move_planes(0)
-        w1_raw1 = shared.tile([P, 2, PACK, H // 2], F32, name="w1_raw1", offset=16384, align_bytes=64)
-        for half in range(2):
-            nc.sync.dma_start(
-                w1_raw1[:, half],
-                w1[512:1024, 256 * half : 256 * half + 256].rearrange("(p j) c -> p j c", j=PACK),
-            )
-        move_planes(1)
 
         picked = {}
 
@@ -144,7 +140,7 @@ def tile_list_residency_ranking_scores_kernel(
                 lhsT=w1_codes[a][:, P * t : P * (t + 1)].bitcast(FP8X4),
                 lhsT_scale=w1_scales[a][:, P * t : P * (t + 1)],
                 rhs=picked[(a, c)].bitcast(FP8X4),
-                rhs_scale=planes[a][:, CHUNK * c : CHUNK * (c + 1)],
+                rhs_scale=planes[a][4 * a : P, CHUNK * c : CHUNK * (c + 1)],
                 start=(a == 0),
                 stop=(a == 1),
             )
@@ -207,15 +203,13 @@ def tile_list_residency_ranking_scores_kernel(
                 )
 
         for pair in ((0, 1), (2, 3)):
-            accs = {}
             for t in pair:
+                accs = [psum.tile([P, CHUNK], F32, name="acc", tag="acc") for c in range(CHUNKS)]
                 for c in range(CHUNKS):
-                    accs[(t, c)] = psum.tile([P, CHUNK], F32, name="acc", tag="acc")
-                    first_pass(accs[(t, c)], 0, t, c)
-            for t in pair:
+                    first_pass(accs[c], 0, t, c)
                 for c in range(CHUNKS):
-                    first_pass(accs[(t, c)], 1, t, c)
-                    nc.scalar.activation(h[t][:, CHUNK * c : CHUNK * (c + 1)], accs[(t, c)][:], ACT.Gelu_apprx_tanh)
+                    first_pass(accs[c], 1, t, c)
+                    nc.scalar.activation(h[t][:, CHUNK * c : CHUNK * (c + 1)], accs[c][:], ACT.Gelu_apprx_tanh)
             for t in pair:
                 nc.vector.tensor_copy(left[t][:], h[t][:].indirect(p1[:]))
                 nc.scalar.activation(gained[t][:], left[t][:], ACT.Copy, scale=gain_sb[:, t : t + 1])

@@ -44,7 +44,7 @@ def tile_list_residency_ranking_scores_kernel(
             nc.sync.dma_start(tile[:].bitcast(I32), tab_words[a].rearrange("p n i -> p (n i)").bitcast(I32))
 
         idx = load_list(offs, "idx")
-        scale_table = keep.tile([P, T], U8, name="scale_table", align_bytes=64)
+        scale_table = shared.tile([P, T], U8, name="scale_table", offset=16384, align_bytes=64)
         nc.sync.dma_start(
             scale_table[0:32, :].bitcast(I32), tab_scales.rearrange("a q t -> (a q) t").bitcast(I32)
         )
@@ -52,35 +52,39 @@ def tile_list_residency_ranking_scores_kernel(
         nc.vector.memset(scale_table[64:128, :].bitcast(I32), 0)
         words0 = keep.tile([P, T], U32, name="words0", align_bytes=64)
         load_words(0, words0)
-        w1_raw0 = keep.tile([P, 1, PACK, H], F32, name="w1_raw0")
-        nc.sync.dma_start(w1_raw0[:, 0], w1[0:512, :].rearrange("(p j) c -> p j c", j=PACK))
-        words1 = shared.tile([P, T], U32, name="words1", offset=0, align_bytes=64)
-        load_words(1, words1)
-        w1_raw1 = shared.tile([P, 2, PACK, H // 2], F32, name="w1_raw1", offset=16384, align_bytes=64)
-        for half in range(2):
-            nc.sync.dma_start(
-                w1_raw1[:, half],
-                w1[512:1024, 256 * half : 256 * half + 256].rearrange("(p j) c -> p j c", j=PACK),
-            )
         p1 = load_list(pos1, "p1")
         p2 = load_list(pos2, "p2")
         p3 = load_list(pos3, "p3")
         p4 = load_list(pos4, "p4")
         p5 = load_list(pos5, "p5")
         p6 = load_list(pos6, "p6")
+        w1_raw0 = keep.tile([P, 1, PACK, H], F32, name="w1_raw0")
+        nc.sync.dma_start(w1_raw0[:, 0], w1[0:512, :].rearrange("(p j) c -> p j c", j=PACK))
 
         planes = [keep.tile([P, S], U8, name="plane%d" % a, align_bytes=64) for a in range(2)]
         for plane in planes:
-            nc.gpsimd.memset(plane[:].bitcast(I32), 0)
+            nc.vector.memset(plane[:].bitcast(I32), 0)
 
         picked_scales = keep.tile([P, S], U8, name="picked_scales", align_bytes=64)
         nc.vector.tensor_copy(picked_scales[:], scale_table[:].indirect(idx[:]))
-        for a, queue in enumerate((nc.gpsimd, nc.sync)):
+
+        def move_planes(a):
             for r in range(4):
-                queue.dma_start(
+                nc.sync.dma_start(
                     planes[a][4 * a + r : P : 32, :].bitcast(I32),
                     picked_scales[16 * a + r : 16 * a + 16 : 4, :].bitcast(I32),
                 )
+
+        words1 = shared.tile([P, T], U32, name="words1", offset=0, align_bytes=64)
+        load_words(1, words1)
+        move_planes(0)
+        w1_raw1 = shared.tile([P, 2, PACK, H // 2], F32, name="w1_raw1", offset=16384, align_bytes=64)
+        for half in range(2):
+            nc.sync.dma_start(
+                w1_raw1[:, half],
+                w1[512:1024, 256 * half : 256 * half + 256].rearrange("(p j) c -> p j c", j=PACK),
+            )
+        move_planes(1)
 
         picked = {}
 
@@ -88,14 +92,14 @@ def tile_list_residency_ranking_scores_kernel(
             nc.vector.tensor_copy(tile[:], window[:].indirect(idx[:, 32 * c : 32 * c + 32]))
             picked[(a, c)] = tile[:]
 
-        def round_w1(raw, rounded):
-            pieces = raw.shape[1]
-            m_piece = P // pieces
-            for piece in range(pieces):
-                nc.scalar.copy(
-                    rounded[:, :, m_piece * piece : m_piece * (piece + 1), :].rearrange("p t m j -> p m j t"),
-                    raw[:, piece].rearrange("p j (m t) -> p m j t", t=PACK),
-                )
+        def round_w1(copy, raw, rounded, m0, m1):
+            m_piece = P // raw.shape[1]
+            piece = m0 // m_piece
+            c0 = PACK * (m0 - piece * m_piece)
+            copy(
+                rounded[:, :, m0:m1, :].rearrange("p t m j -> p m t j"),
+                raw[:, piece, :, c0 : c0 + PACK * (m1 - m0)].rearrange("p j (m t) -> p m t j", t=PACK),
+            )
 
         def quantize_w1(a, t0, t1):
             nc.vector.quantize_mx(
@@ -112,11 +116,15 @@ def tile_list_residency_ranking_scores_kernel(
         nc.vector.tensor_copy(picked0[:], words0[:].indirect(idx[:]))
         for c in range(CHUNKS):
             picked[(0, c)] = picked0[:, CHUNK * c : CHUNK * (c + 1)]
-        round_w1(w1_raw0, w1_bf[0])
+        round_w1(nc.scalar.copy, w1_raw0, w1_bf[0], 0, P)
         quantize_w1(0, 0, 4)
+        picked1 = keep.tile([P, S - CHUNK], U32, name="picked1", align_bytes=64)
+        nc.vector.tensor_copy(picked1[:], words1[:].indirect(idx[:, 0 : (S - CHUNK) // 16]))
         for c in range(CHUNKS - 1):
-            pick_words(1, c, words1, keep.tile([P, CHUNK], U32, name="picked1_%d" % c, align_bytes=64))
-        round_w1(w1_raw1, w1_bf[1])
+            picked[(1, c)] = picked1[:, CHUNK * c : CHUNK * (c + 1)]
+        round_w1(nc.scalar.copy, w1_raw1, w1_bf[1], 0, 64)
+        round_w1(nc.scalar.copy, w1_raw1, w1_bf[1], 64, 104)
+        round_w1(nc.vector.tensor_copy, w1_raw1, w1_bf[1], 104, P)
         quantize_w1(1, 0, 1)
         pick_words(1, CHUNKS - 1, words1, shared.tile([P, CHUNK], U32, name="picked1_last", offset=20480, align_bytes=64))
         quantize_w1(1, 1, 4)
@@ -152,7 +160,7 @@ def tile_list_residency_ranking_scores_kernel(
         minus = [late.tile([P, P2], F32, name="minus%d" % t, offset=2048 * t) for t in range(PACK)]
         a2 = [keep.tile([P, P2], F32, name="a2_%d" % t) for t in range(PACK)]
         a3_lo = late.tile([P, PACK, HALF], F32, name="a3_lo", offset=8192)
-        a3_hi = keep.tile([P, 2, HALF], F32, name="a3_hi")
+        a3_hi = keep.tile([P, PACK, HALF], F32, name="a3_hi")
         a3_bf = [keep.tile([P, HALF, PACK], BF16, name="a3_bf%d" % u, align_bytes=64) for u in range(2)]
         a3_codes = [keep.tile([P, HALF], U32, name="a3_codes%d" % u, align_bytes=64) for u in range(2)]
         a3_scales = [keep.tile([P, HALF], U8, name="a3_scales%d" % u, align_bytes=64) for u in range(2)]
@@ -228,10 +236,11 @@ def tile_list_residency_ranking_scores_kernel(
             pick_hospitals(t, 1)
         for t in (0, 1):
             larger(a3_hi[:, t, :], t, 1)
-        nc.scalar.copy(a3_bf[1][:, :, 0:2], a3_hi[:].rearrange("p t m -> p m t"))
+        nc.scalar.copy(a3_bf[1][:, :, 0:2], a3_hi[:, 0:2].rearrange("p t m -> p m t"))
         scores(0)
         for t in (2, 3):
             pick_hospitals(t, 1)
         for t in (2, 3):
-            larger(a3_bf[1][:, :, t], t, 1)
+            larger(a3_hi[:, t, :], t, 1)
+        nc.vector.tensor_copy(a3_bf[1][:, :, 2:4], a3_hi[:, 2:4].rearrange("p t m -> p m t"))
         scores(1)

from contextlib import ExitStack

import concourse.mybir as mybir

K, H, T, S, N, P1, P2, P3 = 1024, 512, 4096, 2048, 1024, 1024, 512, 256
FLOPS = 2 * K * H * S + 2 * H * N * P3

F32 = mybir.dt.float32
BF16 = mybir.dt.bfloat16
I32 = mybir.dt.int32
U32 = mybir.dt.uint32
U16 = mybir.dt.uint16
U8 = mybir.dt.uint8
FP8X4 = mybir.dt.float8_e4m3fn_x4
FP4X4 = mybir.dt.float4_e2m1fn_x4
ACT = mybir.ActivationFunctionType
ALU = mybir.AluOpType

P = 128
PACK = 4
CHUNK = 512
CHUNKS = S // CHUNK
HALF = P3 // 2
GROUP = 2


def tile_list_residency_ranking_scores_kernel(
    tc, tab_words, tab_scales, offs, w1, pos1, pos2, gain, pos3, pos4, pos5, pos6, lean, w2_words, w2_scales, out
):
    nc = tc.nc
    with ExitStack() as ctx:
        lists = ctx.enter_context(tc.tile_pool(name="lists", bufs=1))
        keep = ctx.enter_context(tc.tile_pool(name="keep", bufs=1))
        shared = ctx.enter_context(tc.tile_pool(name="shared", bufs=1))
        late = ctx.enter_context(tc.tile_pool(name="late", bufs=1))
        psum = ctx.enter_context(tc.psum_pool(name="psum", bufs=8))

        def load_list(src, name):
            tile = lists.tile([P, src.shape[1]], U16, name=name)
            nc.sync.dma_start(tile[:], src)
            return tile

        def load_words(a, tile):
            nc.sync.dma_start(tile[:].bitcast(I32), tab_words[a].rearrange("p n i -> p (n i)").bitcast(I32))

        idx = load_list(offs, "idx")
        scale_table = shared.tile([P, T], U8, name="scale_table", offset=16384, align_bytes=64)
        nc.sync.dma_start(
            scale_table[0:32, :].bitcast(I32), tab_scales.rearrange("a q t -> (a q) t").bitcast(I32)
        )
        nc.vector.memset(scale_table[32:64, :].bitcast(I32), 0)
        nc.vector.memset(scale_table[64:128, :].bitcast(I32), 0)
        words0 = keep.tile([P, T], U32, name="words0", align_bytes=64)
        load_words(0, words0)
        p1 = load_list(pos1, "p1")
        p2 = load_list(pos2, "p2")
        p3 = load_list(pos3, "p3")
        p4 = load_list(pos4, "p4")
        p5 = load_list(pos5, "p5")
        p6 = load_list(pos6, "p6")
        w1_raw0 = keep.tile([P, 1, PACK, H], F32, name="w1_raw0")
        nc.sync.dma_start(w1_raw0[:, 0], w1[0:512, :].rearrange("(p j) c -> p j c", j=PACK))

        planes = [keep.tile([P, S], U8, name="plane%d" % a, align_bytes=64) for a in range(2)]
        for plane in planes:
            nc.vector.memset(plane[:].bitcast(I32), 0)

        picked_scales = keep.tile([P, S], U8, name="picked_scales", align_bytes=64)
        nc.vector.tensor_copy(picked_scales[:], scale_table[:].indirect(idx[:]))

        def move_planes(a):
            for r in range(4):
                nc.sync.dma_start(
                    planes[a][4 * a + r : P : 32, :].bitcast(I32),
                    picked_scales[16 * a + r : 16 * a + 16 : 4, :].bitcast(I32),
                )

        words1 = shared.tile([P, T], U32, name="words1", offset=0, align_bytes=64)
        load_words(1, words1)
        move_planes(0)
        w1_raw1 = shared.tile([P, 2, PACK, H // 2], F32, name="w1_raw1", offset=16384, align_bytes=64)
        for half in range(2):
            nc.sync.dma_start(
                w1_raw1[:, half],
                w1[512:1024, 256 * half : 256 * half + 256].rearrange("(p j) c -> p j c", j=PACK),
            )
        move_planes(1)

        picked = {}

        def pick_words(a, c, window, tile):
            nc.vector.tensor_copy(tile[:], window[:].indirect(idx[:, 32 * c : 32 * c + 32]))
            picked[(a, c)] = tile[:]

        def round_w1(copy, raw, rounded, m0, m1):
            m_piece = P // raw.shape[1]
            piece = m0 // m_piece
            c0 = PACK * (m0 - piece * m_piece)
            copy(
                rounded[:, :, m0:m1, :].rearrange("p t m j -> p m t j"),
                raw[:, piece, :, c0 : c0 + PACK * (m1 - m0)].rearrange("p j (m t) -> p m t j", t=PACK),
            )

        def quantize_w1(a, t0, t1):
            nc.vector.quantize_mx(
                out=w1_codes[a][:, P * t0 : P * t1].bitcast(FP8X4),
                scales=w1_scales[a][:, P * t0 : P * t1],
                in_=w1_bf[a][:, t0:t1].rearrange("p t m j -> p (t m j)"),
            )

        w1_bf = [keep.tile([P, PACK, P, PACK], BF16, name="w1_bf%d" % a, align_bytes=64) for a in range(2)]
        w1_codes = [keep.tile([P, H], U32, name="w1_codes%d" % a, align_bytes=64) for a in range(2)]
        w1_scales = [keep.tile([P, H], U8, name="w1_scales%d" % a, align_bytes=64) for a in range(2)]

        picked0 = keep.tile([P, S], U32, name="picked0", align_bytes=64)
        nc.vector.tensor_copy(picked0[:], words0[:].indirect(idx[:]))
        for c in range(CHUNKS):
            picked[(0, c)] = picked0[:, CHUNK * c : CHUNK * (c + 1)]
        round_w1(nc.scalar.copy, w1_raw0, w1_bf[0], 0, P)
        quantize_w1(0, 0, 4)
        picked1 = keep.tile([P, S - CHUNK], U32, name="picked1", align_bytes=64)
        nc.vector.tensor_copy(picked1[:], words1[:].indirect(idx[:, 0 : (S - CHUNK) // 16]))
        for c in range(CHUNKS - 1):
            picked[(1, c)] = picked1[:, CHUNK * c : CHUNK * (c + 1)]
        round_w1(nc.scalar.copy, w1_raw1, w1_bf[1], 0, 64)
        round_w1(nc.scalar.copy, w1_raw1, w1_bf[1], 64, 104)
        round_w1(nc.vector.tensor_copy, w1_raw1, w1_bf[1], 104, P)
        quantize_w1(1, 0, 1)
        pick_words(1, CHUNKS - 1, words1, shared.tile([P, CHUNK], U32, name="picked1_last", offset=20480, align_bytes=64))
        quantize_w1(1, 1, 4)

        gain_sb = shared.tile([P, PACK], F32, name="gain_sb", offset=0, align_bytes=64)
        nc.sync.dma_start(gain_sb[:], gain.rearrange("(p t) -> p t", t=PACK))
        lean_sb = shared.tile([P, PACK], F32, name="lean_sb", offset=64, align_bytes=64)
        nc.sync.dma_start(lean_sb[:], lean.rearrange("(p t) -> p t", t=PACK))
        w2_codes = shared.tile([P, 2 * N], U8, name="w2_codes", offset=1024, align_bytes=64)
        nc.sync.dma_start(w2_codes[:].bitcast(I32), w2_words[0].bitcast(I32))
        w2_plane = shared.tile([P, N], U8, name="w2_plane", offset=4096, align_bytes=64)
        nc.vector.memset(w2_plane[:].bitcast(I32), 0)
        for q in range(4):
            nc.sync.dma_start(
                w2_plane[32 * q : 32 * q + 4, :].bitcast(I32), w2_scales[0, 4 * q : 4 * q + 4, :].bitcast(I32)
            )

        def first_pass(acc, a, t, c):
            nc.tensor.matmul_mx(
                out=acc[:],
                lhsT=w1_codes[a][:, P * t : P * (t + 1)].bitcast(FP8X4),
                lhsT_scale=w1_scales[a][:, P * t : P * (t + 1)],
                rhs=picked[(a, c)].bitcast(FP8X4),
                rhs_scale=planes[a][4 * a : P, CHUNK * c : CHUNK * (c + 1)],
                start=(a == 0),
                stop=(a == 1),
            )

        h = [keep.tile([P, S], F32, name="h%d" % t) for t in range(PACK)]
        left = [keep.tile([P, P1], F32, name="left%d" % t) for t in range(PACK)]
        gained = [keep.tile([P, P1], F32, name="gained%d" % t) for t in range(PACK)]
        a1 = [keep.tile([P, P1], F32, name="a1_%d" % t) for t in range(PACK)]
        minus = [late.tile([P, P2], F32, name="minus%d" % t, offset=2048 * t) for t in range(PACK)]
        a2 = [keep.tile([P, P2], F32, name="a2_%d" % t) for t in range(PACK)]
        a3_lo = late.tile([P, PACK, HALF], F32, name="a3_lo", offset=8192)
        a3_hi = keep.tile([P, PACK, HALF], F32, name="a3_hi")
        a3_bf = [keep.tile([P, HALF, PACK], BF16, name="a3_bf%d" % u, align_bytes=64) for u in range(2)]
        a3_codes = [keep.tile([P, HALF], U32, name="a3_codes%d" % u, align_bytes=64) for u in range(2)]
        a3_scales = [keep.tile([P, HALF], U8, name="a3_scales%d" % u, align_bytes=64) for u in range(2)]

        hosp = {}

        def pick_hospitals(t, u):
            cols = slice(8 * u, 8 * u + 8)
            for side, places in enumerate((p6, p5)):
                name = "hosp%d_%d_%d" % (t, u, side)
                if u == 0:
                    tile = keep.tile([P, HALF], F32, name=name)
                else:
                    base = 2048 * 3 if t < 2 else 8192
                    tile = late.tile([P, HALF], F32, name=name, offset=base + 512 * (2 * (t % 2) + side))
                nc.vector.tensor_copy(tile[:], a2[t][:].indirect(places[:, cols]))
                hosp[(t, u, side)] = tile

        def larger(dst, t, u):
            nc.vector.scalar_tensor_tensor(
                dst, hosp[(t, u, 0)][:], lean_sb[:, t : t + 1], hosp[(t, u, 1)][:], ALU.mult, ALU.max
            )

        def scores(u):
            nc.vector.quantize_mx(
                out=a3_codes[u][:].bitcast(FP8X4),
                scales=a3_scales[u][:],
                in_=a3_bf[u][:].rearrange("p m t -> p (m t)"),
            )
            for g in range(N // (P * GROUP)):
                acc = psum.tile([P, GROUP, HALF], F32, name="acc", tag="acc")
                for j in range(GROUP):
                    n0 = P * (GROUP * g + j)
                    nc.tensor.matmul_mx(
                        out=acc[:, j, :],
                        lhsT=w2_codes[:, 2 * n0 : 2 * (n0 + P)].bitcast(FP4X4),
                        lhsT_scale=w2_plane[:, n0 : n0 + P],
                        rhs=a3_codes[u][:].bitcast(FP8X4),
                        rhs_scale=a3_scales[u][:],
                        start=True,
                        stop=True,
                    )
                res = keep.tile([P, GROUP, HALF], F32, name="res%d_%d" % (u, g))
                nc.scalar.activation(res[:], acc[:], ACT.Tanh)
                nc.sync.dma_start(
                    out[P * GROUP * g : P * GROUP * (g + 1), HALF * u : HALF * (u + 1)].rearrange("(j p) m -> p j m", p=P),
                    res[:],
                )

        for pair in ((0, 1), (2, 3)):
            for t in pair:
                accs = [psum.tile([P, CHUNK], F32, name="acc", tag="acc") for c in range(CHUNKS)]
                for c in range(CHUNKS):
                    first_pass(accs[c], 0, t, c)
                for c in range(CHUNKS):
                    first_pass(accs[c], 1, t, c)
                    nc.scalar.activation(h[t][:, CHUNK * c : CHUNK * (c + 1)], accs[c][:], ACT.Gelu_apprx_tanh)
            for t in pair:
                nc.vector.tensor_copy(left[t][:], h[t][:].indirect(p1[:]))
                nc.scalar.activation(gained[t][:], left[t][:], ACT.Copy, scale=gain_sb[:, t : t + 1])
            for t in pair:
                nc.vector.tensor_tensor(a1[t][:], h[t][:].indirect(p2[:]), gained[t][:], ALU.mult)
            for t in pair:
                nc.vector.tensor_copy(minus[t][:], a1[t][:].indirect(p4[:]))
            for t in pair:
                nc.vector.tensor_tensor(a2[t][:], a1[t][:].indirect(p3[:]), minus[t][:], ALU.subtract)
            for t in pair:
                pick_hospitals(t, 0)
            for t in pair:
                larger(a3_lo[:, t, :], t, 0)
        nc.scalar.copy(a3_bf[0][:], a3_lo[:].rearrange("p t m -> p m t"))
        for t in (0, 1):
            pick_hospitals(t, 1)
        for t in (0, 1):
            larger(a3_hi[:, t, :], t, 1)
        nc.scalar.copy(a3_bf[1][:, :, 0:2], a3_hi[:, 0:2].rearrange("p t m -> p m t"))
        scores(0)
        for t in (2, 3):
            pick_hospitals(t, 1)
        for t in (2, 3):
            larger(a3_hi[:, t, :], t, 1)
        nc.vector.tensor_copy(a3_bf[1][:, :, 2:4], a3_hi[:, 2:4].rearrange("p t m -> p m t"))
        scores(1)
